import numpy as np
import ml_dtypes


def mxq(x, axis, fmt="e4m3"):
    dtype, down = {"e4m3": (ml_dtypes.float8_e4m3fn, 7), "e5m2": (ml_dtypes.float8_e5m2, 14)}[fmt]
    v = np.moveaxis(np.asarray(x, np.float32).astype(ml_dtypes.bfloat16).astype(np.float64), axis, -1)
    blocks = v.reshape(v.shape[:-1] + (-1, 32))
    amax = np.abs(blocks).max(-1, keepdims=True)
    byte = np.maximum(np.where(amax > 0, np.frexp(amax)[1] - 1 + 127, 0) - down, 1)
    scale = np.exp2(byte - 127.0)
    codes = (blocks / scale).astype(np.float32).astype(dtype).astype(np.float64)
    return np.moveaxis((codes * scale).reshape(v.shape), -1, axis)


WIDE = False


def mx_kscale(k):
    if not WIDE:
        return np.ones(k)
    levels = np.array([10, -10, 5, -5, 0])
    if k % 512:
        return np.exp2(np.random.permutation(np.resize(levels, k // 32))).repeat(32)
    a = np.empty((k // 512, 16))
    for p in range(k // 512):
        a[p, :8] = np.random.permutation(np.resize(levels, 8))
        for g in range(8):
            far = levels[np.abs(levels - a[p, g]) >= 10]
            a[p, g + 8] = far[np.random.randint(len(far))]
    return np.exp2(a.ravel()).repeat(32)


def f64(x):
    return np.asarray(x).astype(np.float64)


def striped8(idx):
    return np.concatenate([x.reshape(-1, 16).T for x in idx]).astype(np.uint16)


def runs(offs, k):
    lists = np.stack([offs[16 * r : 16 * r + 16].T.reshape(-1) for r in range(8)]).astype(np.int64)
    return lists[np.arange(k) % 512 // 64]


def pack_weight(w):
    k, n = w.shape
    w = f64(np.asarray(w, np.float32).astype(ml_dtypes.bfloat16)).reshape(k // 32, 32, n)
    amax = np.abs(w).max(1)
    byte = np.clip(np.where(amax > 0, np.frexp(amax)[1] - 1 + 127 - 7, 1), 1, 254)
    scaled = (w * np.exp2(127.0 - byte)[:, None, :]).reshape(k, n).astype(np.float32)
    words = np.ascontiguousarray(scaled.reshape(k // 512, 128, 4, n).transpose(0, 1, 3, 2)).astype(ml_dtypes.float8_e4m3fn).view(np.uint8)
    return words, np.ascontiguousarray(byte.astype(np.uint8).reshape(k // 512, 16, n))


def unpack_weight(words, scales):
    g, p, n, _ = words.shape
    vals = np.ascontiguousarray(words).view(ml_dtypes.float8_e4m3fn).astype(np.float64) * np.repeat(np.exp2(scales.astype(np.float64) - 127.0), 8, axis=1)[..., None]
    return vals.transpose(0, 1, 3, 2).reshape(g * 512, n)


K, T, S, H, C = 512, 2048, 512, 512, 512


def setup_inputs():
    n = np.random.standard_normal
    s = mx_kscale(K)[:, None]
    packed_xT = pack_weight(n((K, T)) * s)
    return {
        "x_words": packed_xT[0],
        "x_scales": packed_xT[1],
        "w1": (n((K, H)) / np.sqrt(K) / s).astype(np.float32),
        "gs": (np.random.uniform(0.5, 1.5, (K, 1)) / s).astype(np.float32),
        "offs": striped8(np.random.randint(0, T, (8, S))),
        "n1": striped8(np.stack([np.random.permutation(S) for _ in range(8)])),
        "n2": striped8(np.stack([np.random.permutation(S) for _ in range(8)])),
        "n3": striped8(np.stack([np.random.permutation(S) for _ in range(8)])),
        "n4": striped8(np.stack([np.random.permutation(S) for _ in range(8)])),
        "cand": striped8(np.random.randint(0, T, (8, C))),
        "n5": striped8(np.stack([np.random.permutation(S) for _ in range(8)])),
        "n6": striped8(np.stack([np.random.permutation(S) for _ in range(8)])),
        "n7": striped8(np.stack([np.random.permutation(S) for _ in range(8)])),
    }


def reference(x_words, x_scales, w1, gs, offs, n1, n2, n3, n4, cand, n5, n6, n7):
    x_cand = unpack_weight(x_words, x_scales)[np.arange(K)[:, None], runs(cand, K)]
    xq = unpack_weight(x_words, x_scales)[np.arange(K)[:, None], runs(offs, K)]
    y = mxq(f64(w1), 0, "e4m3").T @ xq
    z = f64(gs) * (0.75 * ((y[np.arange(H)[:, None], runs(n1, H)]) * (y[np.arange(H)[:, None], runs(n2, H)]) - ((y[np.arange(H)[:, None], runs(n3, H)]) * (y[np.arange(H)[:, None], runs(n4, H)]))))
    s = 0.0625 * ((x_cand.T @ mxq(z, 0, "e4m3")))
    return 0.75 * (s * (s[np.arange(C)[:, None], runs(n5, C)]) + (s[np.arange(C)[:, None], runs(n6, C)]) * (s[np.arange(C)[:, None], runs(n7, C)]))

@@ -1,0 +1,201 @@
+from contextlib import ExitStack
+
+import concourse.mybir as mybir
+
+F32 = mybir.dt.float32
+BF16 = mybir.dt.bfloat16
+I32 = mybir.dt.int32
+U32 = mybir.dt.uint32
+U16 = mybir.dt.uint16
+U8 = mybir.dt.uint8
+FP8X4 = mybir.dt.float8_e4m3fn_x4
+MULT = mybir.AluOpType.mult
+ADD = mybir.AluOpType.add
+SUB = mybir.AluOpType.subtract
+COPY = mybir.ActivationFunctionType.Copy
+
+P = 128
+PACK = 4
+N = 512
+T = 2048
+FLOPS = 2 * 2 * 512 * 512 * 512
+PIECES = ((0, 256), (256, 384), (384, 512))
+
+
+def tile_picked_hcanddetdot_none_p_kernel(
+    tc, x_words, x_scales, w1, gs, offs, n1, n2, n3, n4, cand, n5, n6, n7, out
+):
+    nc = tc.nc
+    with ExitStack() as ctx:
+        keep = ctx.enter_context(tc.tile_pool(name="keep", bufs=1))
+        ring = ctx.enter_context(tc.tile_pool(name="ring", bufs=2))
+        psum = ctx.enter_context(tc.psum_pool(name="psum", bufs=1))
+
+        def list_tile(name):
+            return keep.tile([P, N // 16], U16, name=name)
+
+        def load_list(name, src):
+            tile = list_tile(name)
+            nc.sync.dma_start(tile[:], src)
+            return tile
+
+        def entries(tile, a, b):
+            return tile[:, a // 16 : b // 16]
+
+        def bank(i):
+            return psum.tile([P, N], F32, name="bank%d" % i, tag="bank%d" % i)
+
+        table_words = keep.tile([P, T], I32, name="table_words", align_bytes=64)
+        table_bytes = keep.tile([P, T], U8, name="table_bytes", align_bytes=64)
+        nc.vector.memset(table_bytes[:].bitcast(I32), 0)
+        nc.sync.dma_start(table_words[:], x_words[0].rearrange("p n t -> p (n t)").bitcast(I32))
+        offs_sb = load_list("offs_sb", offs)
+        nc.sync.dma_start(table_bytes[0:P:8, :].bitcast(I32), x_scales[0].bitcast(I32))
+        cand_sb = load_list("cand_sb", cand)
+        gain = keep.tile([P, PACK], F32, name="gain")
+        nc.scalar.dma_start(gain[:], gs.rearrange("(p t) o -> p (t o)", t=PACK))
+        n1_sb = load_list("n1_sb", n1)
+        w_view = w1.rearrange("(p j) c -> p j c", j=PACK)
+        w_raw = [keep.tile([P, PACK, N // 2], F32, name="w_raw%d" % h) for h in range(2)]
+        for h in range(2):
+            nc.sync.dma_start(w_raw[h][:], w_view[:, :, h * 256 : (h + 1) * 256])
+
+        gain75 = keep.tile([P, PACK], F32, name="gain75")
+        nc.scalar.activation(gain75[:], gain[:], COPY, scale=0.75)
+
+        x_plane = keep.tile([P, N], U8, name="x_plane", align_bytes=64)
+        c_moved = keep.tile([P, N], U8, name="c_moved", align_bytes=64)
+        nc.vector.memset(x_plane[:].bitcast(I32), 0)
+        nc.vector.memset(c_moved[:].bitcast(I32), 0)
+
+        plain = [keep.tile([P, 2 * N if t < 3 else N], F32, name="plain%d" % t) for t in range(PACK)]
+        scaled = [keep.tile([P, 2 * N if t < 3 else N], F32, name="scaled%d" % t) for t in range(PACK)]
+        for t in range(3):
+            nc.gpsimd.memset(scaled[t][:, N:], 0.0)
+            nc.gpsimd.memset(plain[t][:, N:], 0.0)
+
+        def move_rows(queue, dst, src):
+            for c in range(4):
+                queue.dma_start(dst[c:P:32, :].bitcast(I32), src[8 * c : P : 32, :].bitcast(I32))
+
+        x_bytes = keep.tile([P, N], U8, name="x_bytes", align_bytes=64)
+        nc.vector.tensor_copy(x_bytes[:], table_bytes[:].indirect(offs_sb[:]))
+        move_rows(nc.scalar, x_plane, x_bytes)
+        x_codes = keep.tile([P, N], I32, name="x_codes", align_bytes=64)
+        nc.vector.tensor_copy(x_codes[:].bitcast(U32), table_words[:].bitcast(U32).indirect(offs_sb[:]))
+
+        n3_sb = load_list("n3_sb", n3)
+        n2_sb = load_list("n2_sb", n2)
+        n4_sb = load_list("n4_sb", n4)
+
+        c_bytes = keep.tile([P, N], U8, name="c_bytes", align_bytes=64)
+        nc.vector.tensor_copy(c_bytes[:], table_bytes[:].indirect(cand_sb[:]))
+        c_picked = keep.tile([P, N], I32, name="c_picked", align_bytes=64)
+        nc.vector.tensor_copy(c_picked[:].bitcast(U32), table_words[:].bitcast(U32).indirect(cand_sb[:]))
+
+        w_bf = keep.tile([P, PACK * N], BF16, name="w_bf", align_bytes=64)
+        w_dst = w_bf[:].rearrange("p (t m j) -> p m t j", t=PACK, j=PACK)
+
+        def cast_w(engine_copy, h, a, b):
+            src = w_raw[h][:, :, 4 * a : 4 * b].rearrange("p j (m t) -> p m t j", t=PACK)
+            engine_copy(w_dst[:, 64 * h + a : 64 * h + b, :, :], src)
+
+        cast_w(nc.scalar.copy, 0, 0, 64)
+        cast_w(nc.scalar.copy, 1, 0, 24)
+        cast_w(nc.vector.tensor_copy, 1, 24, 64)
+        w_codes = keep.tile([P, N], U32, name="w_codes", align_bytes=64)
+        w_plane = keep.tile([P, N], U8, name="w_plane", align_bytes=64)
+        for a, b in ((0, 128), (128, 256), (256, 512)):
+            nc.vector.quantize_mx(w_codes[:, a:b].bitcast(FP8X4), w_plane[:, a:b], w_bf[:, 4 * a : 4 * b])
+
+        for t in range(PACK):
+            acc = bank(t)
+            cols = slice(P * t, P * (t + 1))
+            nc.tensor.matmul_mx(acc[:], lhsT=w_codes[:, cols].bitcast(FP8X4), lhsT_scale=w_plane[:, cols],
+                                rhs=x_codes[:].bitcast(FP8X4), rhs_scale=x_plane[:], start=True, stop=True)
+            nc.scalar.activation(scaled[t][:, :N], acc[:], COPY, scale=gain75[:, t : t + 1])
+            nc.scalar.copy(plain[t][:, :N], acc[:])
+
+        move_rows(nc.sync, c_moved, c_bytes)
+        n6_sb = load_list("n6_sb", n6)
+        n5_sb = load_list("n5_sb", n5)
+        n7_sb = load_list("n7_sb", n7)
+
+        c_codes = keep.tile([P, N], I32, name="c_codes", align_bytes=64)
+        nc.vector.tensor_copy(
+            c_codes[:].bitcast(U32).rearrange("p (t c i) -> p c t i", t=PACK, i=4),
+            c_picked[:].bitcast(U32).rearrange("p (c i t) -> p c t i", t=PACK, i=4),
+        )
+        c_plane = keep.tile([P, N], U8, name="c_plane", align_bytes=64)
+        nc.vector.tensor_copy(
+            c_plane[:].rearrange("p (t m) -> p t m", t=PACK),
+            c_moved[:].rearrange("p (m t) -> p t m", t=PACK),
+        )
+
+        first = keep.tile([P, PACK * N], F32, name="first")
+        second = keep.tile([P, PACK * N], F32, name="second")
+
+        def y_products(t, a, b):
+            g1 = ring.tile([P, b - a], F32, name="g1")
+            g3 = ring.tile([P, b - a], F32, name="g3")
+            nc.vector.tensor_copy(g1[:], scaled[t][:].indirect(entries(n1_sb, a, b)))
+            nc.vector.tensor_copy(g3[:], scaled[t][:].indirect(entries(n3_sb, a, b)))
+            cols = slice(N * t + a, N * t + b)
+            nc.vector.tensor_tensor(first[:, cols], plain[t][:].indirect(entries(n2_sb, a, b)), g1[:], MULT)
+            nc.vector.tensor_tensor(second[:, cols], plain[t][:].indirect(entries(n4_sb, a, b)), g3[:], MULT)
+
+        s_bank = [None] + [bank(4 + t) for t in range(1, PACK)]
+
+        def z_piece(k, a, b):
+            width = b - a
+            z_bf = keep.tile([P, PACK * width], BF16, name="z_bf%d" % k, align_bytes=64)
+
+            def by_runs(tile):
+                return tile[:].rearrange("p (t c i) -> p c t i", t=PACK, i=4)[:, a // 4 : b // 4, :, :]
+
+            nc.vector.tensor_tensor(
+                z_bf[:].rearrange("p (c i t) -> p c t i", t=PACK, i=4), by_runs(first), by_runs(second), SUB
+            )
+            z_codes = keep.tile([P, width], U32, name="z_codes%d" % k, align_bytes=64)
+            z_plane = keep.tile([P, width], U8, name="z_plane%d" % k, align_bytes=64)
+            nc.vector.quantize_mx(z_codes[:].bitcast(FP8X4), z_plane[:], z_bf[:])
+            for t in range(PACK):
+                cols = slice(P * t, P * (t + 1))
+                dst = bank(k)[:, :width] if t == 0 else s_bank[t][:, a:b]
+                nc.tensor.matmul_mx(dst, lhsT=c_codes[:, cols].bitcast(FP8X4), lhsT_scale=c_plane[:, cols],
+                                    rhs=z_codes[:].bitcast(FP8X4), rhs_scale=z_plane[:], start=True, stop=True)
+                if t == 0:
+                    nc.scalar.activation(plain[0][:, a:b], dst, COPY, scale=0.0625)
+                    nc.scalar.activation(scaled[0][:, a:b], dst, COPY, scale=0.75 * 0.0625)
+
+        for t in range(3):
+            y_products(t, 0, N)
+        for k, (a, b) in enumerate(PIECES):
+            y_products(3, a, b)
+            if k > 0:
+                z_piece(k - 1, *PIECES[k - 1])
+        z_piece(len(PIECES) - 1, *PIECES[-1])
+
+        for t in range(1, PACK):
+            nc.scalar.activation(plain[t][:, :N], s_bank[t][:], COPY, scale=0.0625)
+            nc.scalar.activation(scaled[t][:, :N], s_bank[t][:], COPY, scale=0.75 * 0.0625)
+
+        out_rows = out.rearrange("(p t) j -> t p j", t=PACK)
+        jobs = [(t, 0, N) for t in range(3)] + [(3, a, b) for a, b in PIECES]
+
+        def s_products(t, a, b):
+            g6 = ring.tile([P, b - a], F32, name="g6")
+            p5 = ring.tile([P, b - a], F32, name="p5")
+            p7 = ring.tile([P, b - a], F32, name="p7")
+            nc.vector.tensor_scalar(g6[:], plain[t][:].indirect(entries(n6_sb, a, b)), 0.75, 0.0, MULT, ADD)
+            nc.vector.tensor_tensor(p5[:], plain[t][:].indirect(entries(n5_sb, a, b)), scaled[t][:, a:b], MULT)
+            nc.vector.tensor_tensor(p7[:], plain[t][:].indirect(entries(n7_sb, a, b)), g6[:], MULT)
+            return p5, p7
+
+        def finish(t, a, b, p5, p7):
+            res = ring.tile([P, b - a], F32, name="res", bufs=3)
+            nc.vector.tensor_tensor(res[:], p5[:], p7[:], ADD)
+            nc.sync.dma_start(out_rows[t, :, a:b], res[:])
+
+        for job in jobs:
+            finish(*job, *s_products(*job))

@@ -1,6 +1,7 @@
 from contextlib import ExitStack
 
 import concourse.mybir as mybir
+from concourse.masks import make_identity
 
 F32 = mybir.dt.float32
 BF16 = mybir.dt.bfloat16
@@ -11,15 +12,18 @@ U8 = mybir.dt.uint8
 FP8X4 = mybir.dt.float8_e4m3fn_x4
 MULT = mybir.AluOpType.mult
 ADD = mybir.AluOpType.add
-SUB = mybir.AluOpType.subtract
 COPY = mybir.ActivationFunctionType.Copy
 
 P = 128
 PACK = 4
 N = 512
+HALF = N // 2
 T = 2048
 FLOPS = 2 * 2 * 512 * 512 * 512
-PIECES = ((0, 256), (256, 384), (384, 512))
+CUT = N - P
+Y_WHOLE = 2
+S_WHOLE = 3
+Z_PIECES = ((0, 2 * P), (2 * P, CUT), (CUT, N))
 
 
 def tile_picked_hcanddetdot_none_p_kernel(
@@ -31,11 +35,8 @@ def tile_picked_hcanddetdot_none_p_kernel(
         ring = ctx.enter_context(tc.tile_pool(name="ring", bufs=2))
         psum = ctx.enter_context(tc.psum_pool(name="psum", bufs=1))
 
-        def list_tile(name):
-            return keep.tile([P, N // 16], U16, name=name)
-
         def load_list(name, src):
-            tile = list_tile(name)
+            tile = keep.tile([P, N // 16], U16, name=name)
             nc.sync.dma_start(tile[:], src)
             return tile
 
@@ -45,157 +46,201 @@ def tile_picked_hcanddetdot_none_p_kernel(
         def bank(i):
             return psum.tile([P, N], F32, name="bank%d" % i, tag="bank%d" % i)
 
+        def mx(dst, codes, plane, t, moving_codes, moving_plane):
+            cols = slice(P * t, P * (t + 1))
+            nc.tensor.matmul_mx(dst, lhsT=codes[:, cols].bitcast(FP8X4), lhsT_scale=plane[:, cols],
+                                rhs=moving_codes.bitcast(FP8X4), rhs_scale=moving_plane, start=True, stop=True)
+
         table_words = keep.tile([P, T], I32, name="table_words", align_bytes=64)
         table_bytes = keep.tile([P, T], U8, name="table_bytes", align_bytes=64)
-        nc.vector.memset(table_bytes[:].bitcast(I32), 0)
-        nc.sync.dma_start(table_words[:], x_words[0].rearrange("p n t -> p (n t)").bitcast(I32))
-        offs_sb = load_list("offs_sb", offs)
-        nc.sync.dma_start(table_bytes[0:P:8, :].bitcast(I32), x_scales[0].bitcast(I32))
-        cand_sb = load_list("cand_sb", cand)
+        nc.gpsimd.memset(table_bytes[:].bitcast(I32), 0)
         gain = keep.tile([P, PACK], F32, name="gain")
-        nc.scalar.dma_start(gain[:], gs.rearrange("(p t) o -> p (t o)", t=PACK))
+        nc.gpsimd.dma_start(gain[:], gs.rearrange("(p t) o -> p (t o)", t=PACK))
+        offs_sb = load_list("offs_sb", offs)
+        cand_sb = load_list("cand_sb", cand)
+        for e in range(2):
+            nc.sync.dma_start(table_bytes[e:P:16, :].bitcast(I32), x_scales[0].bitcast(I32)[e:16:2, :])
         n1_sb = load_list("n1_sb", n1)
+        n3_sb = load_list("n3_sb", n3)
         w_view = w1.rearrange("(p j) c -> p j c", j=PACK)
-        w_raw = [keep.tile([P, PACK, N // 2], F32, name="w_raw%d" % h) for h in range(2)]
-        for h in range(2):
-            nc.sync.dma_start(w_raw[h][:], w_view[:, :, h * 256 : (h + 1) * 256])
+        w_raw = [keep.tile([P, PACK, HALF], F32, name="w_raw%d" % h) for h in range(2)]
+        nc.sync.dma_start(w_raw[0][:], w_view[:, :, :HALF])
+        n2_sb = load_list("n2_sb", n2)
+        nc.sync.dma_start(w_raw[1][:], w_view[:, :, HALF:])
+        nc.sync.dma_start(table_words[:], x_words[0].rearrange("p n t -> p (n t)").bitcast(I32))
 
-        gain75 = keep.tile([P, PACK], F32, name="gain75")
-        nc.scalar.activation(gain75[:], gain[:], COPY, scale=0.75)
+        c_plane = keep.tile([P, N], U8, name="c_plane", align_bytes=64)
+        nc.vector.memset(c_plane[:].bitcast(I32), 0)
+        ident = keep.tile([P, P], F32, name="ident")
+        make_identity(nc, ident[:])
 
-        x_plane = keep.tile([P, N], U8, name="x_plane", align_bytes=64)
-        c_moved = keep.tile([P, N], U8, name="c_moved", align_bytes=64)
-        nc.vector.memset(x_plane[:].bitcast(I32), 0)
-        nc.vector.memset(c_moved[:].bitcast(I32), 0)
+        def windows(name, whole):
+            return [keep.tile([P, 2 * N if t < whole else N], F32, name="%s%d" % (name, t)) for t in range(PACK)]
 
-        plain = [keep.tile([P, 2 * N if t < 3 else N], F32, name="plain%d" % t) for t in range(PACK)]
-        scaled = [keep.tile([P, 2 * N if t < 3 else N], F32, name="scaled%d" % t) for t in range(PACK)]
-        for t in range(3):
-            nc.gpsimd.memset(scaled[t][:, N:], 0.0)
-            nc.gpsimd.memset(plain[t][:, N:], 0.0)
-
-        def move_rows(queue, dst, src):
-            for c in range(4):
-                queue.dma_start(dst[c:P:32, :].bitcast(I32), src[8 * c : P : 32, :].bitcast(I32))
+        y_gain, y_plus, y_minus = windows("y_gain", Y_WHOLE), windows("y_plus", Y_WHOLE), windows("y_minus", Y_WHOLE)
+        s_plain, s_scaled = windows("s_plain", S_WHOLE), windows("s_scaled", S_WHOLE)
 
         x_bytes = keep.tile([P, N], U8, name="x_bytes", align_bytes=64)
         nc.vector.tensor_copy(x_bytes[:], table_bytes[:].indirect(offs_sb[:]))
-        move_rows(nc.scalar, x_plane, x_bytes)
-        x_codes = keep.tile([P, N], I32, name="x_codes", align_bytes=64)
-        nc.vector.tensor_copy(x_codes[:].bitcast(U32), table_words[:].bitcast(U32).indirect(offs_sb[:]))
-
-        n3_sb = load_list("n3_sb", n3)
-        n2_sb = load_list("n2_sb", n2)
-        n4_sb = load_list("n4_sb", n4)
-
+        x_plane = keep.tile([P, N], U8, name="x_plane", align_bytes=64)
+        nc.vector.tensor_copy(x_plane[:].bitcast(I32), x_bytes[:].bitcast(I32))
+        for e in range(2):
+            nc.sync.dma_start(x_plane[2 + e : P : 32, :].bitcast(I32), x_bytes[16 + e : P : 32, :].bitcast(I32))
         c_bytes = keep.tile([P, N], U8, name="c_bytes", align_bytes=64)
         nc.vector.tensor_copy(c_bytes[:], table_bytes[:].indirect(cand_sb[:]))
-        c_picked = keep.tile([P, N], I32, name="c_picked", align_bytes=64)
-        nc.vector.tensor_copy(c_picked[:].bitcast(U32), table_words[:].bitcast(U32).indirect(cand_sb[:]))
+        c_dealt = keep.tile([P, N], U8, name="c_dealt", align_bytes=64)
+        nc.vector.tensor_copy(
+            c_dealt[:].rearrange("p (t m) -> p t m", t=PACK),
+            c_bytes[:].rearrange("p (m t) -> p t m", t=PACK),
+        )
+        n4_sb = load_list("n4_sb", n4)
 
         w_bf = keep.tile([P, PACK * N], BF16, name="w_bf", align_bytes=64)
         w_dst = w_bf[:].rearrange("p (t m j) -> p m t j", t=PACK, j=PACK)
-
-        def cast_w(engine_copy, h, a, b):
-            src = w_raw[h][:, :, 4 * a : 4 * b].rearrange("p j (m t) -> p m t j", t=PACK)
-            engine_copy(w_dst[:, 64 * h + a : 64 * h + b, :, :], src)
-
-        cast_w(nc.scalar.copy, 0, 0, 64)
-        cast_w(nc.scalar.copy, 1, 0, 24)
-        cast_w(nc.vector.tensor_copy, 1, 24, 64)
+        for h, cast in enumerate((nc.scalar.copy, nc.vector.tensor_copy)):
+            cast(w_dst[:, 64 * h : 64 * (h + 1), :, :], w_raw[h][:].rearrange("p j (m t) -> p m t j", t=PACK))
         w_codes = keep.tile([P, N], U32, name="w_codes", align_bytes=64)
         w_plane = keep.tile([P, N], U8, name="w_plane", align_bytes=64)
-        for a, b in ((0, 128), (128, 256), (256, 512)):
-            nc.vector.quantize_mx(w_codes[:, a:b].bitcast(FP8X4), w_plane[:, a:b], w_bf[:, 4 * a : 4 * b])
+        nc.vector.quantize_mx(w_codes[:].bitcast(FP8X4), w_plane[:], w_bf[:])
 
-        for t in range(PACK):
+        x_codes = keep.tile([P, N], I32, name="x_codes", align_bytes=64)
+        halves = [slice(0, HALF), slice(HALF, N)]
+        for cols in halves:
+            nc.vector.tensor_copy(
+                x_codes[:].bitcast(U32)[:, cols],
+                table_words[:].bitcast(U32).indirect(entries(offs_sb, cols.start, cols.stop)),
+            )
+
+        def spread_y(t, cols, acc):
+            nc.scalar.activation(y_plus[t][:, cols], acc, COPY, scale=0.75)
+            nc.scalar.activation(y_minus[t][:, cols], acc, COPY, scale=-0.75)
+
+        first_halves = [bank(0), bank(7)]
+        for cols, acc in zip(halves, first_halves):
+            mx(acc[:, :HALF], w_codes, w_plane, 0, x_codes[:, cols], x_plane[:, cols])
+            nc.scalar.activation(y_gain[0][:, cols], acc[:, :HALF], COPY, scale=gain[:, 0:1])
+        for cols, acc in zip(halves, first_halves):
+            spread_y(0, cols, acc[:, :HALF])
+        for t in range(1, PACK):
             acc = bank(t)
-            cols = slice(P * t, P * (t + 1))
-            nc.tensor.matmul_mx(acc[:], lhsT=w_codes[:, cols].bitcast(FP8X4), lhsT_scale=w_plane[:, cols],
-                                rhs=x_codes[:].bitcast(FP8X4), rhs_scale=x_plane[:], start=True, stop=True)
-            nc.scalar.activation(scaled[t][:, :N], acc[:], COPY, scale=gain75[:, t : t + 1])
-            nc.scalar.copy(plain[t][:, :N], acc[:])
+            mx(acc[:], w_codes, w_plane, t, x_codes[:], x_plane[:])
+            nc.scalar.activation(y_gain[t][:, :N], acc[:], COPY, scale=gain[:, t : t + 1])
+            spread_y(t, slice(0, N), acc[:])
 
-        move_rows(nc.sync, c_moved, c_bytes)
-        n6_sb = load_list("n6_sb", n6)
-        n5_sb = load_list("n5_sb", n5)
-        n7_sb = load_list("n7_sb", n7)
-
+        c_picked = keep.tile([P, N], I32, name="c_picked", align_bytes=64)
+        nc.vector.tensor_copy(c_picked[:].bitcast(U32), table_words[:].bitcast(U32).indirect(cand_sb[:]))
         c_codes = keep.tile([P, N], I32, name="c_codes", align_bytes=64)
         nc.vector.tensor_copy(
             c_codes[:].bitcast(U32).rearrange("p (t c i) -> p c t i", t=PACK, i=4),
             c_picked[:].bitcast(U32).rearrange("p (c i t) -> p c t i", t=PACK, i=4),
         )
-        c_plane = keep.tile([P, N], U8, name="c_plane", align_bytes=64)
-        nc.vector.tensor_copy(
-            c_plane[:].rearrange("p (t m) -> p t m", t=PACK),
-            c_moved[:].rearrange("p (m t) -> p t m", t=PACK),
-        )
+        n6_sb = load_list("n6_sb", n6)
+        n5_sb = load_list("n5_sb", n5)
+        n7_sb = load_list("n7_sb", n7)
+        for c in range(4):
+            nc.sync.dma_start(c_plane[c:P:32, :].bitcast(I32), c_dealt[16 * (c // 2) + c % 2 : P : 32, :].bitcast(I32))
 
         first = keep.tile([P, PACK * N], F32, name="first")
         second = keep.tile([P, PACK * N], F32, name="second")
 
+        def add_turned(dst, a, b):
+            nc.tensor.matmul(dst, a, ident[:], is_transpose=True, start=True, stop=False)
+            nc.tensor.matmul(dst, b, ident[:], is_transpose=True, start=False, stop=True)
+
+        blocks = range(CUT // P)
+        z_sum = [bank(4 + jb) for jb in blocks]
+        z_back = [bank(jb) for jb in blocks]
+        z_bf = [keep.tile([P, PACK * (b - a)], BF16, name="z_bf%d" % a, align_bytes=64) for a, b in Z_PIECES]
+
         def y_products(t, a, b):
             g1 = ring.tile([P, b - a], F32, name="g1")
             g3 = ring.tile([P, b - a], F32, name="g3")
-            nc.vector.tensor_copy(g1[:], scaled[t][:].indirect(entries(n1_sb, a, b)))
-            nc.vector.tensor_copy(g3[:], scaled[t][:].indirect(entries(n3_sb, a, b)))
+            nc.vector.tensor_copy(g1[:], y_gain[t][:].indirect(entries(n1_sb, a, b)))
+            nc.vector.tensor_copy(g3[:], y_gain[t][:].indirect(entries(n3_sb, a, b)))
             cols = slice(N * t + a, N * t + b)
-            nc.vector.tensor_tensor(first[:, cols], plain[t][:].indirect(entries(n2_sb, a, b)), g1[:], MULT)
-            nc.vector.tensor_tensor(second[:, cols], plain[t][:].indirect(entries(n4_sb, a, b)), g3[:], MULT)
+            nc.vector.tensor_tensor(first[:, cols], y_plus[t][:].indirect(entries(n2_sb, a, b)), g1[:], MULT)
+            nc.vector.tensor_tensor(second[:, cols], y_minus[t][:].indirect(entries(n4_sb, a, b)), g3[:], MULT)
 
-        s_bank = [None] + [bank(4 + t) for t in range(1, PACK)]
+        def sum_on_tensor(t):
+            for jb in blocks:
+                src = slice(N * t + P * jb, N * t + P * (jb + 1))
+                add_turned(z_sum[jb][:, P * t : P * (t + 1)], first[:, src], second[:, src])
+            if t % 2 == 0:
+                return
+            u = t // 2
+            for jb in blocks:
+                pairs = ring.tile([P, 2 * P], BF16, name="pairs", bufs=3)
+                nc.scalar.copy(
+                    pairs[:].rearrange("j (p e) -> j p e", e=2),
+                    z_sum[jb][:, 2 * P * u : 2 * P * (u + 1)].rearrange("j (e p) -> j p e", e=2),
+                )
+                nc.tensor.transpose(z_back[jb][:, P * u : P * (u + 1)], pairs[:].bitcast(F32), ident[:])
 
-        def z_piece(k, a, b):
-            width = b - a
-            z_bf = keep.tile([P, PACK * width], BF16, name="z_bf%d" % k, align_bytes=64)
-
-            def by_runs(tile):
-                return tile[:].rearrange("p (t c i) -> p c t i", t=PACK, i=4)[:, a // 4 : b // 4, :, :]
-
-            nc.vector.tensor_tensor(
-                z_bf[:].rearrange("p (c i t) -> p c t i", t=PACK, i=4), by_runs(first), by_runs(second), SUB
+        for t in range(PACK):
+            y_products(t, 0, N if t < Y_WHOLE else CUT)
+            sum_on_tensor(t)
+        for jb in blocks:
+            k, lo = (0, 2 * P * jb) if jb < 2 else (1, 0)
+            nc.scalar.copy(
+                z_bf[k][:].bitcast(F32)[:, lo : lo + 2 * P].rearrange("p (j u) -> p j u", u=2),
+                z_back[jb][:, : 2 * P].rearrange("p (u j) -> p j u", u=2),
             )
-            z_codes = keep.tile([P, width], U32, name="z_codes%d" % k, align_bytes=64)
-            z_plane = keep.tile([P, width], U8, name="z_plane%d" % k, align_bytes=64)
-            nc.vector.quantize_mx(z_codes[:].bitcast(FP8X4), z_plane[:], z_bf[:])
-            for t in range(PACK):
-                cols = slice(P * t, P * (t + 1))
-                dst = bank(k)[:, :width] if t == 0 else s_bank[t][:, a:b]
-                nc.tensor.matmul_mx(dst, lhsT=c_codes[:, cols].bitcast(FP8X4), lhsT_scale=c_plane[:, cols],
-                                    rhs=z_codes[:].bitcast(FP8X4), rhs_scale=z_plane[:], start=True, stop=True)
-                if t == 0:
-                    nc.scalar.activation(plain[0][:, a:b], dst, COPY, scale=0.0625)
-                    nc.scalar.activation(scaled[0][:, a:b], dst, COPY, scale=0.75 * 0.0625)
+        for t in range(Y_WHOLE, PACK):
+            y_products(t, CUT, N)
 
-        for t in range(3):
-            y_products(t, 0, N)
-        for k, (a, b) in enumerate(PIECES):
-            y_products(3, a, b)
-            if k > 0:
-                z_piece(k - 1, *PIECES[k - 1])
-        z_piece(len(PIECES) - 1, *PIECES[-1])
+        def by_runs(tile):
+            return tile[:].rearrange("p (t c i) -> p c t i", t=PACK, i=4)[:, CUT // 4 :, :, :]
 
+        nc.vector.tensor_tensor(
+            z_bf[2][:].rearrange("p (c i t) -> p c t i", t=PACK, i=4), by_runs(first), by_runs(second), ADD
+        )
+
+        s_first = [bank(4 + k) for k in range(len(Z_PIECES))]
+        s_bank = [None] + [bank(i) for i in (3, 7, 0)]
+        z_quant = []
+        for k, (a, b) in enumerate(Z_PIECES):
+            z_codes = keep.tile([P, b - a], U32, name="z_codes%d" % k, align_bytes=64)
+            z_plane = keep.tile([P, b - a], U8, name="z_plane%d" % k, align_bytes=64)
+            nc.vector.quantize_mx(z_codes[:].bitcast(FP8X4), z_plane[:], z_bf[k][:])
+            z_quant.append((z_codes, z_plane))
+            mx(s_first[k][:, : b - a], c_codes, c_plane, 0, z_codes[:], z_plane[:])
+            nc.scalar.activation(s_scaled[0][:, a:b], s_first[k][:, : b - a], COPY, scale=0.75 * 0.0625)
+        for k, (a, b) in enumerate(Z_PIECES):
+            nc.scalar.activation(s_plain[0][:, a:b], s_first[k][:, : b - a], COPY, scale=0.0625)
         for t in range(1, PACK):
-            nc.scalar.activation(plain[t][:, :N], s_bank[t][:], COPY, scale=0.0625)
-            nc.scalar.activation(scaled[t][:, :N], s_bank[t][:], COPY, scale=0.75 * 0.0625)
+            for (a, b), (z_codes, z_plane) in zip(Z_PIECES, z_quant):
+                mx(s_bank[t][:, a:b], c_codes, c_plane, t, z_codes[:], z_plane[:])
+            nc.scalar.activation(s_scaled[t][:, :N], s_bank[t][:], COPY, scale=0.75 * 0.0625)
+            nc.scalar.activation(s_plain[t][:, :N], s_bank[t][:], COPY, scale=0.0625)
 
         out_rows = out.rearrange("(p t) j -> t p j", t=PACK)
-        jobs = [(t, 0, N) for t in range(3)] + [(3, a, b) for a, b in PIECES]
 
         def s_products(t, a, b):
             g6 = ring.tile([P, b - a], F32, name="g6")
             p5 = ring.tile([P, b - a], F32, name="p5")
             p7 = ring.tile([P, b - a], F32, name="p7")
-            nc.vector.tensor_scalar(g6[:], plain[t][:].indirect(entries(n6_sb, a, b)), 0.75, 0.0, MULT, ADD)
-            nc.vector.tensor_tensor(p5[:], plain[t][:].indirect(entries(n5_sb, a, b)), scaled[t][:, a:b], MULT)
-            nc.vector.tensor_tensor(p7[:], plain[t][:].indirect(entries(n7_sb, a, b)), g6[:], MULT)
+            nc.vector.tensor_copy(g6[:], s_scaled[t][:].indirect(entries(n6_sb, a, b)))
+            nc.vector.tensor_tensor(p5[:], s_plain[t][:].indirect(entries(n5_sb, a, b)), s_scaled[t][:, a:b], MULT)
+            nc.vector.tensor_tensor(p7[:], s_plain[t][:].indirect(entries(n7_sb, a, b)), g6[:], MULT)
             return p5, p7
 
-        def finish(t, a, b, p5, p7):
+        for t in range(S_WHOLE):
+            p5, p7 = s_products(t, 0, N)
+            sums = bank((1, 2)[t % 2])
+            for jb in range(PACK):
+                cols = slice(P * jb, P * (jb + 1))
+                add_turned(sums[:, cols], p5[:, cols], p7[:, cols])
+            sums_sb = ring.tile([P, N], F32, name="sums_sb")
+            nc.scalar.copy(sums_sb[:], sums[:])
+            back = bank((4, 5)[t % 2])
+            for jb in range(PACK):
+                cols = slice(P * jb, P * (jb + 1))
+                nc.tensor.transpose(back[:, cols], sums_sb[:, cols], ident[:])
+            res = ring.tile([P, N], F32, name="res", bufs=3)
+            nc.scalar.copy(res[:], back[:])
+            nc.sync.dma_start(out_rows[t], res[:])
+        for a, b in ((0, CUT), (CUT, N)):
+            p5, p7 = s_products(PACK - 1, a, b)
             res = ring.tile([P, b - a], F32, name="res", bufs=3)
             nc.vector.tensor_tensor(res[:], p5[:], p7[:], ADD)
-            nc.sync.dma_start(out_rows[t, :, a:b], res[:])
-
-        for job in jobs:
-            finish(*job, *s_products(*job))
+            nc.sync.dma_start(out_rows[PACK - 1, :, a:b], res[:])

@@ -21,7 +21,7 @@ HALF = N // 2
 T = 2048
 FLOPS = 2 * 2 * 512 * 512 * 512
 CUT = N - P
-Y_WHOLE = 2
+Y_WHOLE = 1
 S_WHOLE = 3
 Z_PIECES = ((0, 2 * P), (2 * P, CUT), (CUT, N))
 
@@ -54,8 +54,6 @@ def tile_picked_hcanddetdot_none_p_kernel(
         table_words = keep.tile([P, T], I32, name="table_words", align_bytes=64)
         table_bytes = keep.tile([P, T], U8, name="table_bytes", align_bytes=64)
         nc.gpsimd.memset(table_bytes[:].bitcast(I32), 0)
-        gain = keep.tile([P, PACK], F32, name="gain")
-        nc.gpsimd.dma_start(gain[:], gs.rearrange("(p t) o -> p (t o)", t=PACK))
         offs_sb = load_list("offs_sb", offs)
         cand_sb = load_list("cand_sb", cand)
         for e in range(2):
@@ -68,9 +66,11 @@ def tile_picked_hcanddetdot_none_p_kernel(
         n2_sb = load_list("n2_sb", n2)
         nc.sync.dma_start(w_raw[1][:], w_view[:, :, HALF:])
         nc.sync.dma_start(table_words[:], x_words[0].rearrange("p n t -> p (n t)").bitcast(I32))
+        gain = keep.tile([P, PACK], F32, name="gain")
+        nc.sync.dma_start(gain[:], gs.rearrange("(p t) o -> p (t o)", t=PACK))
 
         c_plane = keep.tile([P, N], U8, name="c_plane", align_bytes=64)
-        nc.vector.memset(c_plane[:].bitcast(I32), 0)
+        nc.gpsimd.memset(c_plane[:].bitcast(I32), 0)
         ident = keep.tile([P, P], F32, name="ident")
         make_identity(nc, ident[:])
 
@@ -197,21 +197,17 @@ def tile_picked_hcanddetdot_none_p_kernel(
 
         s_first = [bank(4 + k) for k in range(len(Z_PIECES))]
         s_bank = [None] + [bank(i) for i in (3, 7, 0)]
-        z_quant = []
+        z_codes = keep.tile([P, N], U32, name="z_codes", align_bytes=64)
+        z_plane = keep.tile([P, N], U8, name="z_plane", align_bytes=64)
         for k, (a, b) in enumerate(Z_PIECES):
-            z_codes = keep.tile([P, b - a], U32, name="z_codes%d" % k, align_bytes=64)
-            z_plane = keep.tile([P, b - a], U8, name="z_plane%d" % k, align_bytes=64)
-            nc.vector.quantize_mx(z_codes[:].bitcast(FP8X4), z_plane[:], z_bf[k][:])
-            z_quant.append((z_codes, z_plane))
-            mx(s_first[k][:, : b - a], c_codes, c_plane, 0, z_codes[:], z_plane[:])
-            nc.scalar.activation(s_scaled[0][:, a:b], s_first[k][:, : b - a], COPY, scale=0.75 * 0.0625)
-        for k, (a, b) in enumerate(Z_PIECES):
+            nc.vector.quantize_mx(z_codes[:, a:b].bitcast(FP8X4), z_plane[:, a:b], z_bf[k][:])
+            mx(s_first[k][:, : b - a], c_codes, c_plane, 0, z_codes[:, a:b], z_plane[:, a:b])
             nc.scalar.activation(s_plain[0][:, a:b], s_first[k][:, : b - a], COPY, scale=0.0625)
+        nc.scalar.activation(s_scaled[0][:, :N], s_plain[0][:, :N], COPY, scale=0.75)
         for t in range(1, PACK):
-            for (a, b), (z_codes, z_plane) in zip(Z_PIECES, z_quant):
-                mx(s_bank[t][:, a:b], c_codes, c_plane, t, z_codes[:], z_plane[:])
-            nc.scalar.activation(s_scaled[t][:, :N], s_bank[t][:], COPY, scale=0.75 * 0.0625)
+            mx(s_bank[t][:], c_codes, c_plane, t, z_codes[:], z_plane[:])
             nc.scalar.activation(s_plain[t][:, :N], s_bank[t][:], COPY, scale=0.0625)
+            nc.scalar.activation(s_scaled[t][:, :N], s_bank[t][:], COPY, scale=0.75 * 0.0625)
 
         out_rows = out.rearrange("(p t) j -> t p j", t=PACK)
 
@@ -219,26 +215,25 @@ def tile_picked_hcanddetdot_none_p_kernel(
             g6 = ring.tile([P, b - a], F32, name="g6")
             p5 = ring.tile([P, b - a], F32, name="p5")
             p7 = ring.tile([P, b - a], F32, name="p7")
-            nc.vector.tensor_copy(g6[:], s_scaled[t][:].indirect(entries(n6_sb, a, b)))
+            nc.vector.tensor_copy(g6[:], s_plain[t][:].indirect(entries(n6_sb, a, b)))
             nc.vector.tensor_tensor(p5[:], s_plain[t][:].indirect(entries(n5_sb, a, b)), s_scaled[t][:, a:b], MULT)
-            nc.vector.tensor_tensor(p7[:], s_plain[t][:].indirect(entries(n7_sb, a, b)), g6[:], MULT)
+            nc.vector.tensor_tensor(p7[:], s_scaled[t][:].indirect(entries(n7_sb, a, b)), g6[:], MULT)
             return p5, p7
 
         for t in range(S_WHOLE):
             p5, p7 = s_products(t, 0, N)
-            sums = bank((1, 2)[t % 2])
-            for jb in range(PACK):
-                cols = slice(P * jb, P * (jb + 1))
-                add_turned(sums[:, cols], p5[:, cols], p7[:, cols])
-            sums_sb = ring.tile([P, N], F32, name="sums_sb")
-            nc.scalar.copy(sums_sb[:], sums[:])
-            back = bank((4, 5)[t % 2])
-            for jb in range(PACK):
-                cols = slice(P * jb, P * (jb + 1))
-                nc.tensor.transpose(back[:, cols], sums_sb[:, cols], ident[:])
-            res = ring.tile([P, N], F32, name="res", bufs=3)
-            nc.scalar.copy(res[:], back[:])
-            nc.sync.dma_start(out_rows[t], res[:])
+            for h, half in enumerate(halves):
+                sums, back = bank(1 + h), bank(4 + h)
+                spans = [(slice(P * i, P * (i + 1)), slice(half.start + P * i, half.start + P * (i + 1))) for i in range(2)]
+                for here, cols in spans:
+                    add_turned(sums[:, here], p5[:, cols], p7[:, cols])
+                sums_sb = ring.tile([P, HALF], F32, name="sums_sb")
+                nc.scalar.copy(sums_sb[:], sums[:, :HALF])
+                for here, cols in spans:
+                    nc.tensor.transpose(back[:, here], sums_sb[:, here], ident[:])
+                res_half = ring.tile([P, HALF], F32, name="res_half", bufs=4)
+                nc.scalar.copy(res_half[:], back[:, :HALF])
+                nc.sync.dma_start(out_rows[t, :, half], res_half[:])
         for a, b in ((0, CUT), (CUT, N)):
             p5, p7 = s_products(PACK - 1, a, b)
             res = ring.tile([P, b - a], F32, name="res", bufs=3)

@@ -62,9 +62,9 @@ def tile_picked_hcanddetdot_none_p_kernel(
         n3_sb = load_list("n3_sb", n3)
         w_view = w1.rearrange("(p j) c -> p j c", j=PACK)
         w_raw = [keep.tile([P, PACK, HALF], F32, name="w_raw%d" % h) for h in range(2)]
-        nc.sync.dma_start(w_raw[0][:], w_view[:, :, :HALF])
-        n2_sb = load_list("n2_sb", n2)
+        nc.scalar.dma_start(w_raw[0][:], w_view[:, :, :HALF])
         nc.sync.dma_start(w_raw[1][:], w_view[:, :, HALF:])
+        n2_sb = load_list("n2_sb", n2)
         nc.sync.dma_start(table_words[:], x_words[0].rearrange("p n t -> p (n t)").bitcast(I32))
         gain = keep.tile([P, PACK], F32, name="gain")
         nc.sync.dma_start(gain[:], gs.rearrange("(p t) o -> p (t o)", t=PACK))
@@ -97,7 +97,7 @@ def tile_picked_hcanddetdot_none_p_kernel(
 
         w_bf = keep.tile([P, PACK * N], BF16, name="w_bf", align_bytes=64)
         w_dst = w_bf[:].rearrange("p (t m j) -> p m t j", t=PACK, j=PACK)
-        for h, cast in enumerate((nc.scalar.copy, nc.vector.tensor_copy)):
+        for h, cast in enumerate((nc.scalar.copy, nc.scalar.copy)):
             cast(w_dst[:, 64 * h : 64 * (h + 1), :, :], w_raw[h][:].rearrange("p j (m t) -> p m t j", t=PACK))
         w_codes = keep.tile([P, N], U32, name="w_codes", align_bytes=64)
         w_plane = keep.tile([P, N], U8, name="w_plane", align_bytes=64)
@@ -150,11 +150,11 @@ def tile_picked_hcanddetdot_none_p_kernel(
         blocks = range(CUT // P)
         z_sum = [bank(4 + jb) for jb in blocks]
         z_back = [bank(jb) for jb in blocks]
-        z_bf = [keep.tile([P, PACK * (b - a)], BF16, name="z_bf%d" % a, align_bytes=64) for a, b in Z_PIECES]
+        z_bf = [keep.tile([P, PACK * (b - a)], BF16, name="z_bf%d" % a, align_bytes=64) for a, b in Z_PIECES[:2]]
 
         def y_products(t, a, b):
-            g1 = ring.tile([P, b - a], F32, name="g1")
-            g3 = ring.tile([P, b - a], F32, name="g3")
+            g1 = ring.tile([P, b - a], F32, name="g1", bufs=1)
+            g3 = ring.tile([P, b - a], F32, name="g3", bufs=1)
             nc.vector.tensor_copy(g1[:], y_gain[t][:].indirect(entries(n1_sb, a, b)))
             nc.vector.tensor_copy(g3[:], y_gain[t][:].indirect(entries(n3_sb, a, b)))
             cols = slice(N * t + a, N * t + b)
@@ -191,18 +191,24 @@ def tile_picked_hcanddetdot_none_p_kernel(
         def by_runs(tile):
             return tile[:].rearrange("p (t c i) -> p c t i", t=PACK, i=4)[:, CUT // 4 :, :, :]
 
-        nc.vector.tensor_tensor(
-            z_bf[2][:].rearrange("p (c i t) -> p c t i", t=PACK, i=4), by_runs(first), by_runs(second), ADD
-        )
-
         s_first = [bank(4 + k) for k in range(len(Z_PIECES))]
         s_bank = [None] + [bank(i) for i in (3, 7, 0)]
         z_codes = keep.tile([P, N], U32, name="z_codes", align_bytes=64)
         z_plane = keep.tile([P, N], U8, name="z_plane", align_bytes=64)
-        for k, (a, b) in enumerate(Z_PIECES):
-            nc.vector.quantize_mx(z_codes[:, a:b].bitcast(FP8X4), z_plane[:, a:b], z_bf[k][:])
+
+        def score_piece(k, values):
+            a, b = Z_PIECES[k]
+            nc.vector.quantize_mx(z_codes[:, a:b].bitcast(FP8X4), z_plane[:, a:b], values[:])
             mx(s_first[k][:, : b - a], c_codes, c_plane, 0, z_codes[:, a:b], z_plane[:, a:b])
             nc.scalar.activation(s_plain[0][:, a:b], s_first[k][:, : b - a], COPY, scale=0.0625)
+
+        score_piece(0, z_bf[0])
+        z_last = keep.tile([P, PACK * P], BF16, name="z_bf0", align_bytes=64)
+        nc.vector.tensor_tensor(
+            z_last[:].rearrange("p (c i t) -> p c t i", t=PACK, i=4), by_runs(first), by_runs(second), ADD
+        )
+        score_piece(1, z_bf[1])
+        score_piece(2, z_last)
         nc.scalar.activation(s_scaled[0][:, :N], s_plain[0][:, :N], COPY, scale=0.75)
         for t in range(1, PACK):
             mx(s_bank[t][:], c_codes, c_plane, t, z_codes[:], z_plane[:])
@@ -211,17 +217,20 @@ def tile_picked_hcanddetdot_none_p_kernel(
 
         out_rows = out.rearrange("(p t) j -> t p j", t=PACK)
 
-        def s_products(t, a, b):
+        def s_fetch(t, a, b):
             g6 = ring.tile([P, b - a], F32, name="g6")
+            nc.vector.tensor_copy(g6[:], s_plain[t][:].indirect(entries(n6_sb, a, b)))
+            return g6
+
+        def s_products(t, a, b, g6):
             p5 = ring.tile([P, b - a], F32, name="p5")
             p7 = ring.tile([P, b - a], F32, name="p7")
-            nc.vector.tensor_copy(g6[:], s_plain[t][:].indirect(entries(n6_sb, a, b)))
             nc.vector.tensor_tensor(p5[:], s_plain[t][:].indirect(entries(n5_sb, a, b)), s_scaled[t][:, a:b], MULT)
             nc.vector.tensor_tensor(p7[:], s_scaled[t][:].indirect(entries(n7_sb, a, b)), g6[:], MULT)
             return p5, p7
 
         for t in range(S_WHOLE):
-            p5, p7 = s_products(t, 0, N)
+            p5, p7 = s_products(t, 0, N, s_fetch(t, 0, N))
             for h, half in enumerate(halves):
                 sums, back = bank(1 + h), bank(4 + h)
                 spans = [(slice(P * i, P * (i + 1)), slice(half.start + P * i, half.start + P * (i + 1))) for i in range(2)]
@@ -234,8 +243,14 @@ def tile_picked_hcanddetdot_none_p_kernel(
                 res_half = ring.tile([P, HALF], F32, name="res_half", bufs=4)
                 nc.scalar.copy(res_half[:], back[:, :HALF])
                 nc.sync.dma_start(out_rows[t, :, half], res_half[:])
-        for a, b in ((0, CUT), (CUT, N)):
-            p5, p7 = s_products(PACK - 1, a, b)
-            res = ring.tile([P, b - a], F32, name="res", bufs=3)
+
+        def finish(a, b, p5, p7):
+            res = ring.tile([P, b - a], F32, name="res")
             nc.vector.tensor_tensor(res[:], p5[:], p7[:], ADD)
             nc.sync.dma_start(out_rows[PACK - 1, :, a:b], res[:])
+
+        last = PACK - 1
+        wide = s_products(last, 0, CUT, s_fetch(last, 0, CUT))
+        g6_end = s_fetch(last, CUT, N)
+        finish(0, CUT, *wide)
+        finish(CUT, N, *s_products(last, CUT, N, g6_end))

@@ -152,14 +152,18 @@ def tile_picked_hcanddetdot_none_p_kernel(
         z_back = [bank(jb) for jb in blocks]
         z_bf = [keep.tile([P, PACK * (b - a)], BF16, name="z_bf%d" % a, align_bytes=64) for a, b in Z_PIECES[:2]]
 
-        def y_products(t, a, b):
-            g1 = ring.tile([P, b - a], F32, name="g1", bufs=1)
-            g3 = ring.tile([P, b - a], F32, name="g3", bufs=1)
-            nc.vector.tensor_copy(g1[:], y_gain[t][:].indirect(entries(n1_sb, a, b)))
-            nc.vector.tensor_copy(g3[:], y_gain[t][:].indirect(entries(n3_sb, a, b)))
-            cols = slice(N * t + a, N * t + b)
-            nc.vector.tensor_tensor(first[:, cols], y_plus[t][:].indirect(entries(n2_sb, a, b)), g1[:], MULT)
-            nc.vector.tensor_tensor(second[:, cols], y_minus[t][:].indirect(entries(n4_sb, a, b)), g3[:], MULT)
+        def y_products(jobs):
+            width = sum(b - a for t, a, b in jobs)
+            g1 = ring.tile([P, width], F32, name="g1", bufs=1)
+            g3 = ring.tile([P, width], F32, name="g3", bufs=1)
+            spans = [slice(i * (b - a), (i + 1) * (b - a)) for i, (t, a, b) in enumerate(jobs)]
+            for span, (t, a, b) in zip(spans, jobs):
+                nc.vector.tensor_copy(g1[:, span], y_gain[t][:].indirect(entries(n1_sb, a, b)))
+                nc.vector.tensor_copy(g3[:, span], y_gain[t][:].indirect(entries(n3_sb, a, b)))
+            for span, (t, a, b) in zip(spans, jobs):
+                cols = slice(N * t + a, N * t + b)
+                nc.vector.tensor_tensor(first[:, cols], y_plus[t][:].indirect(entries(n2_sb, a, b)), g1[:, span], MULT)
+                nc.vector.tensor_tensor(second[:, cols], y_minus[t][:].indirect(entries(n4_sb, a, b)), g3[:, span], MULT)
 
         def sum_on_tensor(t):
             for jb in blocks:
@@ -177,7 +181,7 @@ def tile_picked_hcanddetdot_none_p_kernel(
                 nc.tensor.transpose(z_back[jb][:, P * u : P * (u + 1)], pairs[:].bitcast(F32), ident[:])
 
         for t in range(PACK):
-            y_products(t, 0, N if t < Y_WHOLE else CUT)
+            y_products([(t, 0, N if t < Y_WHOLE else CUT)])
             sum_on_tensor(t)
         for jb in blocks:
             k, lo = (0, 2 * P * jb) if jb < 2 else (1, 0)
@@ -185,8 +189,7 @@ def tile_picked_hcanddetdot_none_p_kernel(
                 z_bf[k][:].bitcast(F32)[:, lo : lo + 2 * P].rearrange("p (j u) -> p j u", u=2),
                 z_back[jb][:, : 2 * P].rearrange("p (u j) -> p j u", u=2),
             )
-        for t in range(Y_WHOLE, PACK):
-            y_products(t, CUT, N)
+        y_products([(t, CUT, N) for t in range(Y_WHOLE, PACK)])
 
         def by_runs(tile):
             return tile[:].rearrange("p (t c i) -> p c t i", t=PACK, i=4)[:, CUT // 4 :, :, :]

from contextlib import ExitStack

import concourse.mybir as mybir
from concourse.masks import make_identity

F32 = mybir.dt.float32
BF16 = mybir.dt.bfloat16
I32 = mybir.dt.int32
U32 = mybir.dt.uint32
U16 = mybir.dt.uint16
U8 = mybir.dt.uint8
FP8X4 = mybir.dt.float8_e4m3fn_x4
MULT = mybir.AluOpType.mult
ADD = mybir.AluOpType.add
COPY = mybir.ActivationFunctionType.Copy

P = 128
PACK = 4
N = 512
HALF = N // 2
T = 2048
FLOPS = 2 * 2 * 512 * 512 * 512
CUT = N - P
Y_WHOLE = 1
S_WHOLE = 3
Z_PIECES = ((0, 2 * P), (2 * P, CUT), (CUT, N))


def tile_picked_hcanddetdot_none_p_kernel(
    tc, x_words, x_scales, w1, gs, offs, n1, n2, n3, n4, cand, n5, n6, n7, out
):
    nc = tc.nc
    with ExitStack() as ctx:
        keep = ctx.enter_context(tc.tile_pool(name="keep", bufs=1))
        ring = ctx.enter_context(tc.tile_pool(name="ring", bufs=2))
        psum = ctx.enter_context(tc.psum_pool(name="psum", bufs=1))

        def load_list(name, src):
            tile = keep.tile([P, N // 16], U16, name=name)
            nc.sync.dma_start(tile[:], src)
            return tile

        def entries(tile, a, b):
            return tile[:, a // 16 : b // 16]

        def bank(i):
            return psum.tile([P, N], F32, name="bank%d" % i, tag="bank%d" % i)

        def mx(dst, codes, plane, t, moving_codes, moving_plane):
            cols = slice(P * t, P * (t + 1))
            nc.tensor.matmul_mx(dst, lhsT=codes[:, cols].bitcast(FP8X4), lhsT_scale=plane[:, cols],
                                rhs=moving_codes.bitcast(FP8X4), rhs_scale=moving_plane, start=True, stop=True)

        table_words = keep.tile([P, T], I32, name="table_words", align_bytes=64)
        table_bytes = keep.tile([P, T], U8, name="table_bytes", align_bytes=64)
        nc.gpsimd.memset(table_bytes[:].bitcast(I32), 0)
        offs_sb = load_list("offs_sb", offs)
        cand_sb = load_list("cand_sb", cand)
        for e in range(2):
            nc.sync.dma_start(table_bytes[e:P:16, :].bitcast(I32), x_scales[0].bitcast(I32)[e:16:2, :])
        n1_sb = load_list("n1_sb", n1)
        n3_sb = load_list("n3_sb", n3)
        w_view = w1.rearrange("(p j) c -> p j c", j=PACK)
        w_raw = [keep.tile([P, PACK, HALF], F32, name="w_raw%d" % h) for h in range(2)]
        nc.scalar.dma_start(w_raw[0][:], w_view[:, :, :HALF])
        nc.sync.dma_start(w_raw[1][:], w_view[:, :, HALF:])
        n2_sb = load_list("n2_sb", n2)
        nc.sync.dma_start(table_words[:], x_words[0].rearrange("p n t -> p (n t)").bitcast(I32))
        gain = keep.tile([P, PACK], F32, name="gain")
        nc.sync.dma_start(gain[:], gs.rearrange("(p t) o -> p (t o)", t=PACK))

        c_plane = keep.tile([P, N], U8, name="c_plane", align_bytes=64)
        nc.gpsimd.memset(c_plane[:].bitcast(I32), 0)
        ident = keep.tile([P, P], F32, name="ident")
        make_identity(nc, ident[:])

        def windows(name, whole):
            return [keep.tile([P, 2 * N if t < whole else N], F32, name="%s%d" % (name, t)) for t in range(PACK)]

        y_gain, y_plus, y_minus = windows("y_gain", Y_WHOLE), windows("y_plus", Y_WHOLE), windows("y_minus", Y_WHOLE)
        s_plain, s_scaled = windows("s_plain", S_WHOLE), windows("s_scaled", S_WHOLE)

        x_bytes = keep.tile([P, N], U8, name="x_bytes", align_bytes=64)
        nc.vector.tensor_copy(x_bytes[:], table_bytes[:].indirect(offs_sb[:]))
        x_plane = keep.tile([P, N], U8, name="x_plane", align_bytes=64)
        nc.vector.tensor_copy(x_plane[:].bitcast(I32), x_bytes[:].bitcast(I32))
        for e in range(2):
            nc.sync.dma_start(x_plane[2 + e : P : 32, :].bitcast(I32), x_bytes[16 + e : P : 32, :].bitcast(I32))
        c_bytes = keep.tile([P, N], U8, name="c_bytes", align_bytes=64)
        nc.vector.tensor_copy(c_bytes[:], table_bytes[:].indirect(cand_sb[:]))
        c_dealt = keep.tile([P, N], U8, name="c_dealt", align_bytes=64)
        nc.vector.tensor_copy(
            c_dealt[:].rearrange("p (t m) -> p t m", t=PACK),
            c_bytes[:].rearrange("p (m t) -> p t m", t=PACK),
        )
        n4_sb = load_list("n4_sb", n4)

        w_bf = keep.tile([P, PACK * N], BF16, name="w_bf", align_bytes=64)
        w_dst = w_bf[:].rearrange("p (t m j) -> p m t j", t=PACK, j=PACK)
        for h, cast in enumerate((nc.scalar.copy, nc.scalar.copy)):
            cast(w_dst[:, 64 * h : 64 * (h + 1), :, :], w_raw[h][:].rearrange("p j (m t) -> p m t j", t=PACK))
        w_codes = keep.tile([P, N], U32, name="w_codes", align_bytes=64)
        w_plane = keep.tile([P, N], U8, name="w_plane", align_bytes=64)
        nc.vector.quantize_mx(w_codes[:].bitcast(FP8X4), w_plane[:], w_bf[:])

        x_codes = keep.tile([P, N], I32, name="x_codes", align_bytes=64)
        halves = [slice(0, HALF), slice(HALF, N)]
        for cols in halves:
            nc.vector.tensor_copy(
                x_codes[:].bitcast(U32)[:, cols],
                table_words[:].bitcast(U32).indirect(entries(offs_sb, cols.start, cols.stop)),
            )

        def spread_y(t, cols, acc):
            nc.scalar.activation(y_plus[t][:, cols], acc, COPY, scale=0.75)
            nc.scalar.activation(y_minus[t][:, cols], acc, COPY, scale=-0.75)

        first_halves = [bank(0), bank(7)]
        for cols, acc in zip(halves, first_halves):
            mx(acc[:, :HALF], w_codes, w_plane, 0, x_codes[:, cols], x_plane[:, cols])
            nc.scalar.activation(y_gain[0][:, cols], acc[:, :HALF], COPY, scale=gain[:, 0:1])
        for cols, acc in zip(halves, first_halves):
            spread_y(0, cols, acc[:, :HALF])
        for t in range(1, PACK):
            acc = bank(t)
            mx(acc[:], w_codes, w_plane, t, x_codes[:], x_plane[:])
            nc.scalar.activation(y_gain[t][:, :N], acc[:], COPY, scale=gain[:, t : t + 1])
            spread_y(t, slice(0, N), acc[:])

        c_picked = keep.tile([P, N], I32, name="c_picked", align_bytes=64)
        nc.vector.tensor_copy(c_picked[:].bitcast(U32), table_words[:].bitcast(U32).indirect(cand_sb[:]))
        c_codes = keep.tile([P, N], I32, name="c_codes", align_bytes=64)
        nc.vector.tensor_copy(
            c_codes[:].bitcast(U32).rearrange("p (t c i) -> p c t i", t=PACK, i=4),
            c_picked[:].bitcast(U32).rearrange("p (c i t) -> p c t i", t=PACK, i=4),
        )
        n6_sb = load_list("n6_sb", n6)
        n5_sb = load_list("n5_sb", n5)
        n7_sb = load_list("n7_sb", n7)
        for c in range(4):
            nc.sync.dma_start(c_plane[c:P:32, :].bitcast(I32), c_dealt[16 * (c // 2) + c % 2 : P : 32, :].bitcast(I32))

        first = keep.tile([P, PACK * N], F32, name="first")
        second = keep.tile([P, PACK * N], F32, name="second")

        def add_turned(dst, a, b):
            nc.tensor.matmul(dst, a, ident[:], is_transpose=True, start=True, stop=False)
            nc.tensor.matmul(dst, b, ident[:], is_transpose=True, start=False, stop=True)

        blocks = range(CUT // P)
        z_sum = [bank(4 + jb) for jb in blocks]
        z_back = [bank(jb) for jb in blocks]
        z_bf = [keep.tile([P, PACK * (b - a)], BF16, name="z_bf%d" % a, align_bytes=64) for a, b in Z_PIECES[:2]]

        def y_products(jobs):
            width = sum(b - a for t, a, b in jobs)
            g1 = ring.tile([P, width], F32, name="g1", bufs=1)
            g3 = ring.tile([P, width], F32, name="g3", bufs=1)
            spans = [slice(i * (b - a), (i + 1) * (b - a)) for i, (t, a, b) in enumerate(jobs)]
            for span, (t, a, b) in zip(spans, jobs):
                nc.vector.tensor_copy(g1[:, span], y_gain[t][:].indirect(entries(n1_sb, a, b)))
                nc.vector.tensor_copy(g3[:, span], y_gain[t][:].indirect(entries(n3_sb, a, b)))
            for span, (t, a, b) in zip(spans, jobs):
                cols = slice(N * t + a, N * t + b)
                nc.vector.tensor_tensor(first[:, cols], y_plus[t][:].indirect(entries(n2_sb, a, b)), g1[:, span], MULT)
                nc.vector.tensor_tensor(second[:, cols], y_minus[t][:].indirect(entries(n4_sb, a, b)), g3[:, span], MULT)

        def sum_on_tensor(t):
            for jb in blocks:
                src = slice(N * t + P * jb, N * t + P * (jb + 1))
                add_turned(z_sum[jb][:, P * t : P * (t + 1)], first[:, src], second[:, src])
            if t % 2 == 0:
                return
            u = t // 2
            for jb in blocks:
                pairs = ring.tile([P, 2 * P], BF16, name="pairs", bufs=3)
                nc.scalar.copy(
                    pairs[:].rearrange("j (p e) -> j p e", e=2),
                    z_sum[jb][:, 2 * P * u : 2 * P * (u + 1)].rearrange("j (e p) -> j p e", e=2),
                )
                nc.tensor.transpose(z_back[jb][:, P * u : P * (u + 1)], pairs[:].bitcast(F32), ident[:])

        for t in range(PACK):
            y_products([(t, 0, N if t < Y_WHOLE else CUT)])
            sum_on_tensor(t)
        for jb in blocks:
            k, lo = (0, 2 * P * jb) if jb < 2 else (1, 0)
            nc.scalar.copy(
                z_bf[k][:].bitcast(F32)[:, lo : lo + 2 * P].rearrange("p (j u) -> p j u", u=2),
                z_back[jb][:, : 2 * P].rearrange("p (u j) -> p j u", u=2),
            )
        y_products([(t, CUT, N) for t in range(Y_WHOLE, PACK)])

        def by_runs(tile):
            return tile[:].rearrange("p (t c i) -> p c t i", t=PACK, i=4)[:, CUT // 4 :, :, :]

        s_first = [bank(4 + k) for k in range(len(Z_PIECES))]
        s_bank = [None] + [bank(i) for i in (3, 7, 0)]
        z_codes = keep.tile([P, N], U32, name="z_codes", align_bytes=64)
        z_plane = keep.tile([P, N], U8, name="z_plane", align_bytes=64)

        def score_piece(k, values):
            a, b = Z_PIECES[k]
            nc.vector.quantize_mx(z_codes[:, a:b].bitcast(FP8X4), z_plane[:, a:b], values[:])
            mx(s_first[k][:, : b - a], c_codes, c_plane, 0, z_codes[:, a:b], z_plane[:, a:b])
            nc.scalar.activation(s_plain[0][:, a:b], s_first[k][:, : b - a], COPY, scale=0.0625)

        score_piece(0, z_bf[0])
        z_last = keep.tile([P, PACK * P], BF16, name="z_bf0", align_bytes=64)
        nc.vector.tensor_tensor(
            z_last[:].rearrange("p (c i t) -> p c t i", t=PACK, i=4), by_runs(first), by_runs(second), ADD
        )
        score_piece(1, z_bf[1])
        score_piece(2, z_last)
        nc.scalar.activation(s_scaled[0][:, :N], s_plain[0][:, :N], COPY, scale=0.75)
        for t in range(1, PACK):
            mx(s_bank[t][:], c_codes, c_plane, t, z_codes[:], z_plane[:])
            nc.scalar.activation(s_plain[t][:, :N], s_bank[t][:], COPY, scale=0.0625)
            nc.scalar.activation(s_scaled[t][:, :N], s_bank[t][:], COPY, scale=0.75 * 0.0625)

        out_rows = out.rearrange("(p t) j -> t p j", t=PACK)

        def s_fetch(t, a, b):
            g6 = ring.tile([P, b - a], F32, name="g6")
            nc.vector.tensor_copy(g6[:], s_plain[t][:].indirect(entries(n6_sb, a, b)))
            return g6

        def s_products(t, a, b, g6):
            p5 = ring.tile([P, b - a], F32, name="p5")
            p7 = ring.tile([P, b - a], F32, name="p7")
            nc.vector.tensor_tensor(p5[:], s_plain[t][:].indirect(entries(n5_sb, a, b)), s_scaled[t][:, a:b], MULT)
            nc.vector.tensor_tensor(p7[:], s_scaled[t][:].indirect(entries(n7_sb, a, b)), g6[:], MULT)
            return p5, p7

        for t in range(S_WHOLE):
            p5, p7 = s_products(t, 0, N, s_fetch(t, 0, N))
            for h, half in enumerate(halves):
                sums, back = bank(1 + h), bank(4 + h)
                spans = [(slice(P * i, P * (i + 1)), slice(half.start + P * i, half.start + P * (i + 1))) for i in range(2)]
                for here, cols in spans:
                    add_turned(sums[:, here], p5[:, cols], p7[:, cols])
                sums_sb = ring.tile([P, HALF], F32, name="sums_sb")
                nc.scalar.copy(sums_sb[:], sums[:, :HALF])
                for here, cols in spans:
                    nc.tensor.transpose(back[:, here], sums_sb[:, here], ident[:])
                res_half = ring.tile([P, HALF], F32, name="res_half", bufs=4)
                nc.scalar.copy(res_half[:], back[:, :HALF])
                nc.sync.dma_start(out_rows[t, :, half], res_half[:])

        def finish(a, b, p5, p7):
            res = ring.tile([P, b - a], F32, name="res")
            nc.vector.tensor_tensor(res[:], p5[:], p7[:], ADD)
            nc.sync.dma_start(out_rows[PACK - 1, :, a:b], res[:])

        last = PACK - 1
        wide = s_products(last, 0, CUT, s_fetch(last, 0, CUT))
        g6_end = s_fetch(last, CUT, N)
        finish(0, CUT, *wide)
        finish(CUT, N, *s_products(last, CUT, N, g6_end))
